import numpy as np
import ml_dtypes


def mxq(x, axis, fmt="e4m3"):
    dtype, down = {"e4m3": (ml_dtypes.float8_e4m3fn, 7), "e5m2": (ml_dtypes.float8_e5m2, 14)}[fmt]
    v = np.moveaxis(np.asarray(x, np.float32).astype(ml_dtypes.bfloat16).astype(np.float64), axis, -1)
    blocks = v.reshape(v.shape[:-1] + (-1, 32))
    amax = np.abs(blocks).max(-1, keepdims=True)
    byte = np.maximum(np.where(amax > 0, np.frexp(amax)[1] - 1 + 127, 0) - down, 1)
    scale = np.exp2(byte - 127.0)
    codes = (blocks / scale).astype(np.float32).astype(dtype).astype(np.float64)
    return np.moveaxis((codes * scale).reshape(v.shape), -1, axis)


WIDE = False


def mx_kscale(k):
    if not WIDE:
        return np.ones(k)
    levels = np.array([10, -10, 5, -5, 0])
    if k % 512:
        return np.exp2(np.random.permutation(np.resize(levels, k // 32))).repeat(32)
    a = np.empty((k // 512, 16))
    for p in range(k // 512):
        a[p, :8] = np.random.permutation(np.resize(levels, 8))
        for g in range(8):
            far = levels[np.abs(levels - a[p, g]) >= 10]
            a[p, g + 8] = far[np.random.randint(len(far))]
    return np.exp2(a.ravel()).repeat(32)


def f64(x):
    return np.asarray(x).astype(np.float64)


def striped(idx):
    return np.tile(np.asarray(idx).reshape(-1, 16).T, (8, 1)).astype(np.uint16)


def unstriped(offs):
    return offs[:16].T.reshape(-1).astype(np.int64)


E2M1 = np.array([0.0, 0.5, 1.0, 1.5, 2.0, 3.0, 4.0, 6.0, -0.0, -0.5, -1.0, -1.5, -2.0, -3.0, -4.0, -6.0])


def pack_weight(w, fmt):
    k, n = w.shape
    w = f64(np.asarray(w, np.float32).astype(ml_dtypes.bfloat16)).reshape(k // 32, 32, n)
    amax = np.abs(w).max(1)
    if fmt == "e4m3":
        byte = np.frexp(amax)[1] - 1 + 127 - 7
    else:
        mant, ex = np.frexp(amax / 6.0)
        byte = np.where(mant > 0.5, ex, ex - 1) + 127
    byte = np.clip(np.where(amax > 0, byte, 1), 1, 254)
    scaled = (w * np.exp2(127.0 - byte)[:, None, :]).reshape(k, n).astype(np.float32)
    by_word = np.ascontiguousarray(scaled.reshape(k // 512, 128, 4, n).transpose(0, 1, 3, 2))
    if fmt == "e4m3":
        words = by_word.astype(ml_dtypes.float8_e4m3fn).view(np.uint8)
    else:
        c = by_word.astype(ml_dtypes.float4_e2m1fn).view(np.uint8) & 0xF
        words = (c[..., 0::2] | (c[..., 1::2] << 4)).reshape(k // 512, 128, 2 * n)
    return np.ascontiguousarray(words), np.ascontiguousarray(byte.astype(np.uint8).reshape(k // 512, 16, n))


def unpack_weight(words, scales, fmt):
    g, _, n = scales.shape
    words = np.ascontiguousarray(words).reshape(g, 128, n, -1)
    if fmt == "e4m3":
        vals = words.view(ml_dtypes.float8_e4m3fn).astype(np.float64)
    else:
        nib = np.empty((g, 128, n, 4), np.uint8)
        nib[..., 0::2] = words & 0xF
        nib[..., 1::2] = words >> 4
        vals = E2M1[nib]
    vals = vals * np.repeat(np.exp2(scales.astype(np.float64) - 127.0), 8, axis=1)[..., None]
    return vals.transpose(0, 1, 3, 2).reshape(g * 512, n)


def sigmoid(v):
    return 1.0 / (1.0 + np.exp(-v))


K, T, J, R, N = 1024, 1024, 512, 512, 512


def setup_inputs():
    n = np.random.standard_normal
    idx = np.random.permutation(T)[:J]
    idx2 = np.random.permutation(T)[:J]
    fk = mx_kscale(K)
    fr = mx_kscale(R)
    xtp = pack_weight(n((K, T)) / fk[:, None], "e4m3")
    wap = pack_weight(n((K, R)) * 1 / np.sqrt(K) * fk[:, None], "e2m1")
    wcp = pack_weight(n((K, R)) * 1 / np.sqrt(K) * fk[:, None], "e4m3")
    wgp = pack_weight(n((K, R)) * 1 / np.sqrt(K) * fk[:, None], "e2m1")
    wbp = pack_weight(n((R, N)) * 1 / np.sqrt(R) / fr[:, None], "e4m3")
    return {
        "xt_words": xtp[0],
        "xt_scales": xtp[1],
        "wa_words": wap[0],
        "wa_scales": wap[1],
        "wc_words": wcp[0],
        "wc_scales": wcp[1],
        "wg_words": wgp[0],
        "wg_scales": wgp[1],
        "us": (np.random.uniform(0.5, 2.0, (R, 1)) * fr[:, None]).astype(np.float32),
        "wb_words": wbp[0],
        "wb_scales": wbp[1],
        "rw": (np.random.uniform(0.5, 2.0, (1, J))).astype(np.float32),
        "offs": striped(idx),
        "offs2": striped(idx2),
    }


def reference(xt_words, xt_scales, wa_words, wa_scales, wc_words, wc_scales, wg_words, wg_scales, us, wb_words, wb_scales, rw, offs, offs2):
    idx = unstriped(offs)
    idx2 = unstriped(offs2)
    xtu = unpack_weight(xt_words, xt_scales, "e4m3")
    wau = unpack_weight(wa_words, wa_scales, "e2m1")
    wcu = unpack_weight(wc_words, wc_scales, "e4m3")
    wgu = unpack_weight(wg_words, wg_scales, "e2m1")
    wbu = unpack_weight(wb_words, wb_scales, "e4m3")
    xtidxg = xtu[:, idx]
    a = wau.T @ xtidxg
    xtidx2g = xtu[:, idx2]
    b = wcu.T @ xtidx2g
    g = wgu.T @ xtidxg
    hid = (b + sigmoid(g) * (a - b)) * f64(us)
    hidq = mxq(hid, 0, "e4m3")
    p = wbu.T @ hidq
    y = p * f64(rw)
    return y

@@ -1,0 +1,262 @@
+from contextlib import ExitStack
+
+import concourse.mybir as mybir
+from concourse.masks import make_identity
+
+K, T, J, R, N = 1024, 1024, 512, 512, 512
+FLOPS = 2 * (3 * K * R * J + R * N * J)
+
+F32 = mybir.dt.float32
+BF16 = mybir.dt.bfloat16
+I32 = mybir.dt.int32
+U32 = mybir.dt.uint32
+U16 = mybir.dt.uint16
+U8 = mybir.dt.uint8
+FP8X4 = mybir.dt.float8_e4m3fn_x4
+FP4X4 = mybir.dt.float4_e2m1fn_x4
+MULT = mybir.AluOpType.mult
+SIGMOID = mybir.ActivationFunctionType.Sigmoid
+
+P = 128
+PACK = 4
+PASSES = 2
+BLOCKS = J // P
+HALF = J // 2
+BANKS = {"g": ("x", 3), "turned": ("x", 3), "a": ("y", 3), "p": ("y", 3), "b": ("z", 2)}
+
+
+def tile_moe_expert_hidden_gated_pair_kernel(
+    tc, xt_words, xt_scales, wa_words, wa_scales, wc_words, wc_scales, wg_words, wg_scales,
+    us, wb_words, wb_scales, rw, offs, offs2, out,
+):
+    nc = tc.nc
+    with ExitStack() as ctx:
+        keep = ctx.enter_context(tc.tile_pool(name="keep", bufs=1))
+        ring = ctx.enter_context(tc.tile_pool(name="ring", bufs=4))
+        psum = ctx.enter_context(tc.psum_pool(name="psum", bufs=1))
+
+        def held(name, shape, dtype):
+            return keep.tile(shape, dtype, name=name, align_bytes=64)
+
+        def bank(name, shape):
+            return psum.tile(shape, F32, name=name, tag=BANKS[name][0], bufs=BANKS[name][1])
+
+        list1 = held("list1", [P, J // 16], U16)
+        list2 = held("list2", [P, J // 16], U16)
+        x_words = held("x_words", [P, PASSES, T], I32)
+        x_plane = held("x_plane", [P, T], U8)
+        wa_w = held("wa_w", [P, PASSES, 2 * R], U8)
+        wg_w = held("wg_w", [P, PASSES, 2 * R], U8)
+        wc_w = held("wc_w", [P, PASSES, R], I32)
+        wb_w = held("wb_w", [P, N], I32)
+        wa_s = held("wa_s", [P, PASSES, R], U8)
+        wg_s = held("wg_s", [P, PASSES, R], U8)
+        wc_s = held("wc_s", [P, R], U8)
+        wb_s = held("wb_s", [P, N], U8)
+        s1 = held("s1", [P, J], U8)
+        s1_low = held("s1_low", [P, J], U8)
+        s2 = held("s2", [P, J], U8)
+        us_sb = held("us_sb", [P, PACK], F32)
+        rw_all = held("rw_all", [P, J], F32)
+        ident = held("ident", [P, P], F32)
+        warm_in = held("warm_in", [P, 1], F32)
+        warm_out = held("warm_out", [P, 1], F32)
+
+        nc.gpsimd.memset(x_plane[:].bitcast(I32), 0)
+        for t in (wa_s, wg_s):
+            nc.vector.memset(t[:].rearrange("p z c -> p (z c)").bitcast(I32), 0)
+        for t in (wc_s, s1_low, wb_s):
+            nc.vector.memset(t[:].bitcast(I32), 0)
+        nc.gpsimd.memset(warm_in[:], 0.0)
+        nc.scalar.activation(out=warm_out[:], in_=warm_in[:], func=SIGMOID)
+        make_identity(nc, ident[:])
+
+        def words_i32(w, z):
+            return w[z].rearrange("p n t -> p (n t)").bitcast(I32)
+
+        def load_packed(tile, scales, queue):
+            for q in range(4):
+                queue.dma_start(
+                    out=tile[32 * q : 32 * q + 4 * scales.shape[0], :].bitcast(I32),
+                    in_=scales[:, 4 * q : 4 * q + 4, :].bitcast(I32),
+                )
+
+        def load_side_by_side(tile, scales, queue):
+            for q in range(4):
+                queue.dma_start(
+                    out=tile[32 * q : 32 * q + 4, :, :].bitcast(I32),
+                    in_=scales[:, 4 * q : 4 * q + 4, :].rearrange("z q c -> q z c").bitcast(I32),
+                )
+
+        load_packed(x_plane, xt_scales, nc.sync)
+        nc.sync.dma_start(list1[:], offs)
+        nc.sync.dma_start(list2[:], offs2)
+        nc.sync.dma_start(out=x_words[:], in_=xt_words.rearrange("z p n t -> p z (n t)").bitcast(I32))
+        nc.sync.dma_start(out=wg_w[:].bitcast(I32), in_=wg_words.rearrange("z p c -> p z c").bitcast(I32))
+        load_side_by_side(wg_s, wg_scales, nc.sync)
+        nc.sync.dma_start(out=wa_w[:].bitcast(I32), in_=wa_words.rearrange("z p c -> p z c").bitcast(I32))
+        load_side_by_side(wa_s, wa_scales, nc.gpsimd)
+        nc.sync.dma_start(out=wc_w[:], in_=wc_words.rearrange("z p n t -> p z (n t)").bitcast(I32))
+        load_packed(wc_s, wc_scales, nc.sync)
+        nc.sync.dma_start(out=us_sb[:], in_=us.rearrange("(p t) o -> p (t o)", t=PACK))
+        nc.sync.dma_start(out=wb_w[:], in_=words_i32(wb_words, 0))
+        nc.sync.dma_start(out=rw_all[:], in_=rw[0].partition_broadcast(P))
+        load_packed(wb_s, wb_scales, nc.gpsimd)
+
+        gathered = {}
+
+        def gather_words(which, z, h):
+            g = held("xg%d%d%d" % (which, z, h), [P, HALF], I32)
+            lst = (list1, list2)[which]
+            cols = HALF // 16
+            nc.vector.tensor_copy(
+                g[:].bitcast(U32), x_words[:, z, :].bitcast(U32).indirect(lst[:, h * cols : (h + 1) * cols])
+            )
+            gathered[(which, z, h)] = g
+
+        nc.vector.tensor_copy(s1[:], x_plane[:].indirect(list1[:]))
+        nc.scalar.dma_start(out=s1_low[0:112, :].bitcast(I32), in_=s1[4:116, :].bitcast(I32))
+        nc.vector.tensor_copy(s2[:], x_plane[:].indirect(list2[:]))
+        gather_words(0, 0, 0)
+        gather_words(0, 1, 0)
+        gather_words(1, 0, 0)
+        gather_words(1, 1, 0)
+        gather_words(0, 0, 1)
+        gather_words(0, 1, 1)
+        gather_words(1, 0, 1)
+        gather_words(1, 1, 1)
+
+
+        acc = {}
+        val = {}
+
+        def tokens(which, z, i):
+            g = gathered[(which, z, i // 2)]
+            return g[:, (i % 2) * P : (i % 2 + 1) * P].bitcast(FP8X4)
+
+        def fp4_pass(name, w, ws, z, i):
+            if z == 0:
+                acc[(name, i)] = bank(name, [P, R])
+            plane = (s1, s1_low)[z]
+            nc.tensor.matmul_mx(
+                out=acc[(name, i)][:], lhsT=tokens(0, z, i), lhsT_scale=plane[:, i * P : (i + 1) * P],
+                rhs=w[:, z, :].bitcast(FP4X4), rhs_scale=ws[:, z, :], start=(z == 0), stop=(z == PASSES - 1),
+            )
+
+        def ga(i, z):
+            fp4_pass("g", wg_w, wg_s, z, i)
+            fp4_pass("a", wa_w, wa_s, z, i)
+
+        def bmm(i):
+            acc[("b", i)] = bank("b", [P, R])
+            for z in range(PASSES):
+                nc.tensor.matmul_mx(
+                    out=acc[("b", i)][:], lhsT=tokens(1, z, i), lhsT_scale=s2[4 * z : P, i * P : (i + 1) * P],
+                    rhs=wc_w[:, z, :].bitcast(FP8X4), rhs_scale=wc_s[4 * z : P, :],
+                    start=(z == 0), stop=(z == PASSES - 1),
+                )
+
+        def by_slot(name, i):
+            return acc[(name, i)][:].rearrange("p (m t) -> p t m", t=PACK)
+
+        def sig(i):
+            for name, sign in (("s", 1.0), ("sn", -1.0)):
+                t = ring.tile([P, PACK, P], F32, name=name)
+                nc.scalar.activation(out=t[:], in_=by_slot("g", i), func=SIGMOID, scale=sign)
+                val[(name, i)] = t
+
+        def prod(name, src, gate, i):
+            t = ring.tile([P, PACK, P], F32, name=name)
+            nc.vector.tensor_tensor(out=t[:], in0=by_slot(src, i), in1=val[(gate, i)][:], op=MULT)
+            val[(name, i)] = t
+
+        def turn(i):
+            tb = bank("turned", [P, PACK, P])
+            for t in range(PACK):
+                nc.tensor.matmul(tb[:, t, :], val[("u", i)][:, t, :], ident[:], start=True, stop=False, is_transpose=True)
+                nc.tensor.matmul(tb[:, t, :], val[("v", i)][:, t, :], ident[:], start=False, stop=True, is_transpose=True)
+            acc[("t", i)] = tb
+
+        def hid(i):
+            h = ring.tile([P, P, PACK], BF16, name="hid", align_bytes=64)
+            nc.vector.tensor_tensor(
+                out=h[:], in0=acc[("t", i)][:].rearrange("p t j -> p j t"),
+                in1=us_sb[:].unsqueeze(1).to_broadcast([P, P, PACK]), op=MULT,
+            )
+            val[("h", i)] = h
+
+        def quant(i):
+            codes = ring.tile([P, P], U32, name="codes", align_bytes=64)
+            plane = ring.tile([P, P], U8, name="plane", align_bytes=64)
+            nc.vector.quantize_mx(out=codes[:].bitcast(FP8X4), scales=plane[:], in_=val[("h", i)][:].rearrange("p j t -> p (j t)"))
+            val[("q", i)] = (codes, plane)
+
+        def second(i):
+            pb = bank("p", [P, N // P, P])
+            codes, plane = val[("q", i)]
+            for nb in range(N // P):
+                cols = slice(nb * P, (nb + 1) * P)
+                nc.tensor.matmul_mx(
+                    out=pb[:, nb, :], lhsT=wb_w[:, cols].bitcast(FP8X4), lhsT_scale=wb_s[:, cols],
+                    rhs=codes[:].bitcast(FP8X4), rhs_scale=plane[:], start=True, stop=True,
+                )
+            acc[("p", i)] = pb
+
+        def finish(i):
+            y = ring.tile([P, N // P, P], F32, name="y")
+            cols = slice(i * P, (i + 1) * P)
+            nc.vector.tensor_tensor(
+                out=y[:], in0=acc[("p", i)][:], in1=rw_all[:, cols].unsqueeze(1).to_broadcast([P, N // P, P]), op=MULT,
+            )
+            nc.sync.dma_start(out=out.rearrange("(nb p) j -> p nb j", p=P)[:, :, cols], in_=y[:])
+
+        def u(i):
+            prod("u", "a", "s", i)
+
+        def v(i):
+            prod("v", "b", "sn", i)
+
+        ga(0, 0)
+        ga(1, 0)
+        ga(0, 1)
+        sig(0)
+        ga(1, 1)
+        sig(1)
+        bmm(0)
+        bmm(1)
+        ga(2, 0)
+        ga(2, 1)
+        sig(2)
+        u(0)
+        v(0)
+        ga(3, 0)
+        ga(3, 1)
+        sig(3)
+        u(1)
+        v(1)
+        turn(0)
+        bmm(2)
+        u(2)
+        turn(1)
+        bmm(3)
+        hid(0)
+        v(2)
+        quant(0)
+        u(3)
+        hid(1)
+        turn(2)
+        second(0)
+        v(3)
+        quant(1)
+        turn(3)
+        second(1)
+        hid(2)
+        finish(0)
+        quant(2)
+        second(2)
+        hid(3)
+        finish(1)
+        quant(3)
+        second(3)
+        finish(2)
+        finish(3)

@@ -15,14 +15,19 @@ U8 = mybir.dt.uint8
 FP8X4 = mybir.dt.float8_e4m3fn_x4
 FP4X4 = mybir.dt.float4_e2m1fn_x4
 MULT = mybir.AluOpType.mult
+SUBTRACT = mybir.AluOpType.subtract
 SIGMOID = mybir.ActivationFunctionType.Sigmoid
 
 P = 128
 PACK = 4
-PASSES = 2
+PASSES = K // (P * PACK)
+QUADRANTS = 4
+ROWS = 4
 BLOCKS = J // P
 HALF = J // 2
-BANKS = {"g": ("x", 3), "turned": ("x", 3), "a": ("y", 3), "p": ("y", 3), "b": ("z", 2)}
+OUT_TILES = N // P
+LIFTED = 112
+SECOND_LAG = 3
 
 
 def tile_moe_expert_hidden_gated_pair_kernel(
@@ -32,19 +37,19 @@ def tile_moe_expert_hidden_gated_pair_kernel(
     nc = tc.nc
     with ExitStack() as ctx:
         keep = ctx.enter_context(tc.tile_pool(name="keep", bufs=1))
-        ring = ctx.enter_context(tc.tile_pool(name="ring", bufs=4))
+        ring = ctx.enter_context(tc.tile_pool(name="ring", bufs=BLOCKS))
         psum = ctx.enter_context(tc.psum_pool(name="psum", bufs=1))
 
         def held(name, shape, dtype):
             return keep.tile(shape, dtype, name=name, align_bytes=64)
 
-        def bank(name, shape):
-            return psum.tile(shape, F32, name=name, tag=BANKS[name][0], bufs=BANKS[name][1])
+        def bank(name, number, shape):
+            return psum.tile(shape, F32, name=name, tag="bank%d" % number)
 
         list1 = held("list1", [P, J // 16], U16)
         list2 = held("list2", [P, J // 16], U16)
-        x_words = held("x_words", [P, PASSES, T], I32)
-        x_plane = held("x_plane", [P, T], U8)
+        x_words = held("x_words", [P, PASSES * T], I32)
+        x_scales = held("x_scales", [P, T], U8)
         wa_w = held("wa_w", [P, PASSES, 2 * R], U8)
         wg_w = held("wg_w", [P, PASSES, 2 * R], U8)
         wc_w = held("wc_w", [P, PASSES, R], I32)
@@ -53,210 +58,175 @@ def tile_moe_expert_hidden_gated_pair_kernel(
         wg_s = held("wg_s", [P, PASSES, R], U8)
         wc_s = held("wc_s", [P, R], U8)
         wb_s = held("wb_s", [P, N], U8)
-        s1 = held("s1", [P, J], U8)
-        s1_low = held("s1_low", [P, J], U8)
-        s2 = held("s2", [P, J], U8)
+        token_s = held("token_s", [P, J], U8)
+        token_s_pass1 = held("token_s_pass1", [P, J], U8)
+        context_s = held("context_s", [P, J], U8)
         us_sb = held("us_sb", [P, PACK], F32)
         rw_all = held("rw_all", [P, J], F32)
         ident = held("ident", [P, P], F32)
-        warm_in = held("warm_in", [P, 1], F32)
-        warm_out = held("warm_out", [P, 1], F32)
 
-        nc.gpsimd.memset(x_plane[:].bitcast(I32), 0)
-        for t in (wa_s, wg_s):
-            nc.vector.memset(t[:].rearrange("p z c -> p (z c)").bitcast(I32), 0)
-        for t in (wc_s, s1_low, wb_s):
-            nc.vector.memset(t[:].bitcast(I32), 0)
-        nc.gpsimd.memset(warm_in[:], 0.0)
-        nc.scalar.activation(out=warm_out[:], in_=warm_in[:], func=SIGMOID)
+        nc.gpsimd.memset(x_scales[:].bitcast(I32), 0)
+        nc.vector.memset(wc_s[:].bitcast(I32), 0)
+        for tile in (wg_s, wa_s):
+            nc.vector.memset(tile[:].rearrange("p z c -> p (z c)").bitcast(I32), 0)
+        for tile in (token_s_pass1, wb_s):
+            nc.vector.memset(tile[:].bitcast(I32), 0)
         make_identity(nc, ident[:])
 
-        def words_i32(w, z):
-            return w[z].rearrange("p n t -> p (n t)").bitcast(I32)
+        def load_stacked(queue, tile, scales, q):
+            queue.dma_start(
+                out=tile[32 * q : 32 * q + ROWS * scales.shape[0], :].bitcast(I32),
+                in_=scales[:, ROWS * q : ROWS * (q + 1), :].bitcast(I32),
+            )
 
-        def load_packed(tile, scales, queue):
-            for q in range(4):
-                queue.dma_start(
-                    out=tile[32 * q : 32 * q + 4 * scales.shape[0], :].bitcast(I32),
-                    in_=scales[:, 4 * q : 4 * q + 4, :].bitcast(I32),
-                )
+        def load_beside(tile, scales, q):
+            nc.sync.dma_start(
+                out=tile[32 * q : 32 * q + ROWS, :, :].bitcast(I32),
+                in_=scales[:, ROWS * q : ROWS * (q + 1), :].rearrange("z q c -> q z c").bitcast(I32),
+            )
 
-        def load_side_by_side(tile, scales, queue):
-            for q in range(4):
-                queue.dma_start(
-                    out=tile[32 * q : 32 * q + 4, :, :].bitcast(I32),
-                    in_=scales[:, 4 * q : 4 * q + 4, :].rearrange("z q c -> q z c").bitcast(I32),
-                )
+        def load_x_pass(z):
+            nc.sync.dma_start(
+                out=x_words[:, z * T : (z + 1) * T], in_=xt_words[z].rearrange("p n t -> p (n t)").bitcast(I32)
+            )
 
-        load_packed(x_plane, xt_scales, nc.sync)
+        def load_fp4(tile, words):
+            nc.sync.dma_start(out=tile[:].bitcast(I32), in_=words.rearrange("z p c -> p z c").bitcast(I32))
+
+        for q in range(QUADRANTS):
+            load_stacked(nc.sync, x_scales, xt_scales, q)
         nc.sync.dma_start(list1[:], offs)
+        load_x_pass(0)
         nc.sync.dma_start(list2[:], offs2)
-        nc.sync.dma_start(out=x_words[:], in_=xt_words.rearrange("z p n t -> p z (n t)").bitcast(I32))
-        nc.sync.dma_start(out=wg_w[:].bitcast(I32), in_=wg_words.rearrange("z p c -> p z c").bitcast(I32))
-        load_side_by_side(wg_s, wg_scales, nc.sync)
-        nc.sync.dma_start(out=wa_w[:].bitcast(I32), in_=wa_words.rearrange("z p c -> p z c").bitcast(I32))
-        load_side_by_side(wa_s, wa_scales, nc.gpsimd)
+        load_fp4(wg_w, wg_words)
+        for q in range(QUADRANTS):
+            load_beside(wg_s, wg_scales, q)
+        load_x_pass(1)
+        load_fp4(wa_w, wa_words)
+        for q in range(QUADRANTS // 2):
+            load_stacked(nc.gpsimd, wc_s, wc_scales, q)
+
+        nc.vector.tensor_copy(token_s[:], x_scales[:].indirect(list1[:]))
+        nc.sync.dma_start(out=token_s_pass1[0:LIFTED, :].bitcast(I32), in_=token_s[ROWS : ROWS + LIFTED, :].bitcast(I32))
+
         nc.sync.dma_start(out=wc_w[:], in_=wc_words.rearrange("z p n t -> p z (n t)").bitcast(I32))
-        load_packed(wc_s, wc_scales, nc.sync)
+        for q in range(QUADRANTS):
+            load_beside(wa_s, wa_scales, q)
+            if q >= QUADRANTS // 2:
+                load_stacked(nc.sync, wc_s, wc_scales, q)
         nc.sync.dma_start(out=us_sb[:], in_=us.rearrange("(p t) o -> p (t o)", t=PACK))
-        nc.sync.dma_start(out=wb_w[:], in_=words_i32(wb_words, 0))
+        nc.sync.dma_start(out=wb_w[:], in_=wb_words[0].rearrange("p n t -> p (n t)").bitcast(I32))
+        for q in range(QUADRANTS):
+            load_stacked(nc.sync, wb_s, wb_scales, q)
         nc.sync.dma_start(out=rw_all[:], in_=rw[0].partition_broadcast(P))
-        load_packed(wb_s, wb_scales, nc.gpsimd)
 
-        gathered = {}
-
-        def gather_words(which, z, h):
-            g = held("xg%d%d%d" % (which, z, h), [P, HALF], I32)
-            lst = (list1, list2)[which]
-            cols = HALF // 16
+        def gather_words(name, offsets, window, half):
+            words = held(name, [P, HALF], I32)
+            columns = HALF // 16
             nc.vector.tensor_copy(
-                g[:].bitcast(U32), x_words[:, z, :].bitcast(U32).indirect(lst[:, h * cols : (h + 1) * cols])
+                words[:].bitcast(U32), window.bitcast(U32).indirect(offsets[:, half * columns : (half + 1) * columns])
             )
-            gathered[(which, z, h)] = g
+            return words
 
-        nc.vector.tensor_copy(s1[:], x_plane[:].indirect(list1[:]))
-        nc.scalar.dma_start(out=s1_low[0:112, :].bitcast(I32), in_=s1[4:116, :].bitcast(I32))
-        nc.vector.tensor_copy(s2[:], x_plane[:].indirect(list2[:]))
-        gather_words(0, 0, 0)
-        gather_words(0, 1, 0)
-        gather_words(1, 0, 0)
-        gather_words(1, 1, 0)
-        gather_words(0, 0, 1)
-        gather_words(0, 1, 1)
-        gather_words(1, 0, 1)
-        gather_words(1, 1, 1)
+        token_w = {}
+        context_w = {}
+        for half in range(2):
+            token_w[0, half] = gather_words("token_w0%d" % half, list1, x_words[:, 0:T], half)
+        nc.vector.tensor_copy(context_s[:], x_scales[:].indirect(list2[:]))
+        for half in range(2):
+            token_w[1, half] = gather_words("token_w1%d" % half, list1, x_words[:, T : 2 * T], half)
+        for half in range(2):
+            context_w[0, half] = gather_words("context_w0%d" % half, list2, x_words[:], half)
+            context_w[1, half] = gather_words("context_w1%d" % half, list2, x_words[:, T : 2 * T], half)
 
+        def slots(i):
+            return slice(i * P, (i + 1) * P)
 
-        acc = {}
-        val = {}
+        def stationary(words, z, i):
+            return words[z, i // 2][:, slots(i % 2)].bitcast(FP8X4)
 
-        def tokens(which, z, i):
-            g = gathered[(which, z, i // 2)]
-            return g[:, (i % 2) * P : (i % 2 + 1) * P].bitcast(FP8X4)
-
-        def fp4_pass(name, w, ws, z, i):
-            if z == 0:
-                acc[(name, i)] = bank(name, [P, R])
-            plane = (s1, s1_low)[z]
+        def fp4_pass(acc, w, w_s, z, i):
             nc.tensor.matmul_mx(
-                out=acc[(name, i)][:], lhsT=tokens(0, z, i), lhsT_scale=plane[:, i * P : (i + 1) * P],
-                rhs=w[:, z, :].bitcast(FP4X4), rhs_scale=ws[:, z, :], start=(z == 0), stop=(z == PASSES - 1),
+                out=acc[:], lhsT=stationary(token_w, z, i), lhsT_scale=(token_s, token_s_pass1)[z][:, slots(i)],
+                rhs=w[:, z, :].bitcast(FP4X4), rhs_scale=w_s[:, z, :], start=(z == 0), stop=(z == PASSES - 1),
             )
 
-        def ga(i, z):
-            fp4_pass("g", wg_w, wg_s, z, i)
-            fp4_pass("a", wa_w, wa_s, z, i)
+        def by_t(acc):
+            return acc[:].rearrange("p (m t) -> p t m", t=PACK)
 
-        def bmm(i):
-            acc[("b", i)] = bank("b", [P, R])
+        g_acc = [bank("g", i, [P, R]) for i in range(BLOCKS)]
+        gate = []
+        for i in range(BLOCKS):
+            fp4_pass(g_acc[i], wg_w, wg_s, 0, i)
+        for i in range(BLOCKS):
+            fp4_pass(g_acc[i], wg_w, wg_s, 1, i)
+            s = ring.tile([P, PACK, P], F32, name="s")
+            nc.scalar.activation(out=s[:], in_=by_t(g_acc[i]), func=SIGMOID)
+            gate.append(s)
+
+        terms = {}
+        quantised = {}
+
+        def first_layer(i):
+            a = bank("a", BLOCKS + i, [P, R])
+            for z in range(PASSES):
+                fp4_pass(a, wa_w, wa_s, z, i)
+            b = bank("b", i, [P, R])
             for z in range(PASSES):
                 nc.tensor.matmul_mx(
-                    out=acc[("b", i)][:], lhsT=tokens(1, z, i), lhsT_scale=s2[4 * z : P, i * P : (i + 1) * P],
-                    rhs=wc_w[:, z, :].bitcast(FP8X4), rhs_scale=wc_s[4 * z : P, :],
+                    out=b[:], lhsT=stationary(context_w, z, i), lhsT_scale=context_s[ROWS * z : P, slots(i)],
+                    rhs=wc_w[:, z, :].bitcast(FP8X4), rhs_scale=wc_s[ROWS * z : P, :],
                     start=(z == 0), stop=(z == PASSES - 1),
                 )
+            a_term = ring.tile([P, PACK, P], F32, name="a_term")
+            nc.vector.scalar_tensor_tensor(out=a_term[:], in0=gate[i][:], scalar=-1.0, in1=by_t(a), op0=MULT, op1=MULT)
+            b_term = ring.tile([P, PACK, P], F32, name="b_term")
+            nc.vector.scalar_tensor_tensor(out=b_term[:], in0=gate[i][:], scalar=1.0, in1=by_t(b), op0=SUBTRACT, op1=MULT)
+            terms[i] = (a_term, b_term)
 
-        def by_slot(name, i):
-            return acc[(name, i)][:].rearrange("p (m t) -> p t m", t=PACK)
-
-        def sig(i):
-            for name, sign in (("s", 1.0), ("sn", -1.0)):
-                t = ring.tile([P, PACK, P], F32, name=name)
-                nc.scalar.activation(out=t[:], in_=by_slot("g", i), func=SIGMOID, scale=sign)
-                val[(name, i)] = t
-
-        def prod(name, src, gate, i):
-            t = ring.tile([P, PACK, P], F32, name=name)
-            nc.vector.tensor_tensor(out=t[:], in0=by_slot(src, i), in1=val[(gate, i)][:], op=MULT)
-            val[(name, i)] = t
-
-        def turn(i):
-            tb = bank("turned", [P, PACK, P])
-            for t in range(PACK):
-                nc.tensor.matmul(tb[:, t, :], val[("u", i)][:, t, :], ident[:], start=True, stop=False, is_transpose=True)
-                nc.tensor.matmul(tb[:, t, :], val[("v", i)][:, t, :], ident[:], start=False, stop=True, is_transpose=True)
-            acc[("t", i)] = tb
-
-        def hid(i):
-            h = ring.tile([P, P, PACK], BF16, name="hid", align_bytes=64)
-            nc.vector.tensor_tensor(
-                out=h[:], in0=acc[("t", i)][:].rearrange("p t j -> p j t"),
-                in1=us_sb[:].unsqueeze(1).to_broadcast([P, P, PACK]), op=MULT,
+        def hidden(i):
+            turned = bank("turned", BLOCKS + i, [P, PACK, P])
+            for n_term, term in enumerate(terms[i]):
+                for t in range(PACK):
+                    nc.tensor.matmul(
+                        turned[:, t, :], term[:, t, :], ident[:], is_transpose=True,
+                        start=(n_term == 0 and t == 0), stop=(n_term == 1 and t == PACK - 1),
+                    )
+            hid = ring.tile([P, P, PACK], BF16, name="hid", align_bytes=64)
+            nc.vector.scalar_tensor_tensor(
+                out=hid[:], in0=turned[:].rearrange("p t j -> p j t"), scalar=-1.0,
+                in1=us_sb[:].unsqueeze(1).to_broadcast([P, P, PACK]), op0=MULT, op1=MULT,
             )
-            val[("h", i)] = h
-
-        def quant(i):
             codes = ring.tile([P, P], U32, name="codes", align_bytes=64)
-            plane = ring.tile([P, P], U8, name="plane", align_bytes=64)
-            nc.vector.quantize_mx(out=codes[:].bitcast(FP8X4), scales=plane[:], in_=val[("h", i)][:].rearrange("p j t -> p (j t)"))
-            val[("q", i)] = (codes, plane)
+            scales = ring.tile([P, P], U8, name="scales", align_bytes=64)
+            nc.vector.quantize_mx(out=codes[:].bitcast(FP8X4), scales=scales[:], in_=hid[:].rearrange("p j t -> p (j t)"))
+            quantised[i] = (codes, scales)
 
-        def second(i):
-            pb = bank("p", [P, N // P, P])
-            codes, plane = val[("q", i)]
-            for nb in range(N // P):
-                cols = slice(nb * P, (nb + 1) * P)
+        out_tiles = out.rearrange("(nb p) j -> p nb j", p=P)
+
+        def second_layer(i):
+            codes, scales = quantised[i]
+            sums = bank("sums", i, [P, OUT_TILES, P])
+            for nb in range(OUT_TILES):
                 nc.tensor.matmul_mx(
-                    out=pb[:, nb, :], lhsT=wb_w[:, cols].bitcast(FP8X4), lhsT_scale=wb_s[:, cols],
-                    rhs=codes[:].bitcast(FP8X4), rhs_scale=plane[:], start=True, stop=True,
+                    out=sums[:, nb, :], lhsT=wb_w[:, slots(nb)].bitcast(FP8X4), lhsT_scale=wb_s[:, slots(nb)],
+                    rhs=codes[:].bitcast(FP8X4), rhs_scale=scales[:], start=True, stop=True,
                 )
-            acc[("p", i)] = pb
+            queues = (nc.sync, nc.scalar) if i == BLOCKS - 1 else (nc.sync,)
+            width = OUT_TILES // len(queues)
+            for part, queue in enumerate(queues):
+                tiles = slice(part * width, (part + 1) * width)
+                y = ring.tile([P, width, P], F32, name="y%d" % part)
+                nc.vector.tensor_tensor(
+                    out=y[:], in0=sums[:, tiles, :], in1=rw_all[:, slots(i)].unsqueeze(1).to_broadcast([P, width, P]),
+                    op=MULT,
+                )
+                queue.dma_start(out=out_tiles[:, tiles, slots(i)], in_=y[:])
 
-        def finish(i):
-            y = ring.tile([P, N // P, P], F32, name="y")
-            cols = slice(i * P, (i + 1) * P)
-            nc.vector.tensor_tensor(
-                out=y[:], in0=acc[("p", i)][:], in1=rw_all[:, cols].unsqueeze(1).to_broadcast([P, N // P, P]), op=MULT,
-            )
-            nc.sync.dma_start(out=out.rearrange("(nb p) j -> p nb j", p=P)[:, :, cols], in_=y[:])
-
-        def u(i):
-            prod("u", "a", "s", i)
-
-        def v(i):
-            prod("v", "b", "sn", i)
-
-        ga(0, 0)
-        ga(1, 0)
-        ga(0, 1)
-        sig(0)
-        ga(1, 1)
-        sig(1)
-        bmm(0)
-        bmm(1)
-        ga(2, 0)
-        ga(2, 1)
-        sig(2)
-        u(0)
-        v(0)
-        ga(3, 0)
-        ga(3, 1)
-        sig(3)
-        u(1)
-        v(1)
-        turn(0)
-        bmm(2)
-        u(2)
-        turn(1)
-        bmm(3)
-        hid(0)
-        v(2)
-        quant(0)
-        u(3)
-        hid(1)
-        turn(2)
-        second(0)
-        v(3)
-        quant(1)
-        turn(3)
-        second(1)
-        hid(2)
-        finish(0)
-        quant(2)
-        second(2)
-        hid(3)
-        finish(1)
-        quant(3)
-        second(3)
-        finish(2)
-        finish(3)
+        for step in range(BLOCKS + SECOND_LAG):
+            if step < BLOCKS:
+                first_layer(step)
+            if 1 <= step <= BLOCKS:
+                hidden(step - 1)
+            if step >= SECOND_LAG:
+                second_layer(step - SECOND_LAG)

@@ -28,6 +28,7 @@ HALF = J // 2
 OUT_TILES = N // P
 LIFTED = 112
 SECOND_LAG = 3
+A_LEAD = 2
 
 
 def tile_moe_expert_hidden_gated_pair_kernel(
@@ -103,17 +104,15 @@ def tile_moe_expert_hidden_gated_pair_kernel(
             load_beside(wg_s, wg_scales, q)
         load_x_pass(1)
         load_fp4(wa_w, wa_words)
-        for q in range(QUADRANTS // 2):
+        for q in range(QUADRANTS):
             load_stacked(nc.gpsimd, wc_s, wc_scales, q)
 
         nc.vector.tensor_copy(token_s[:], x_scales[:].indirect(list1[:]))
         nc.sync.dma_start(out=token_s_pass1[0:LIFTED, :].bitcast(I32), in_=token_s[ROWS : ROWS + LIFTED, :].bitcast(I32))
 
-        nc.sync.dma_start(out=wc_w[:], in_=wc_words.rearrange("z p n t -> p z (n t)").bitcast(I32))
         for q in range(QUADRANTS):
             load_beside(wa_s, wa_scales, q)
-            if q >= QUADRANTS // 2:
-                load_stacked(nc.sync, wc_s, wc_scales, q)
+        nc.sync.dma_start(out=wc_w[:], in_=wc_words.rearrange("z p n t -> p z (n t)").bitcast(I32))
         nc.sync.dma_start(out=us_sb[:], in_=us.rearrange("(p t) o -> p (t o)", t=PACK))
         nc.sync.dma_start(out=wb_w[:], in_=wb_words[0].rearrange("p n t -> p (n t)").bitcast(I32))
         for q in range(QUADRANTS):
@@ -164,13 +163,16 @@ def tile_moe_expert_hidden_gated_pair_kernel(
             nc.scalar.activation(out=s[:], in_=by_t(g_acc[i]), func=SIGMOID)
             gate.append(s)
 
+        a_acc = {}
         terms = {}
         quantised = {}
 
-        def first_layer(i):
-            a = bank("a", BLOCKS + i, [P, R])
+        def product_a(i):
+            a_acc[i] = bank("a", BLOCKS + i, [P, R])
             for z in range(PASSES):
-                fp4_pass(a, wa_w, wa_s, z, i)
+                fp4_pass(a_acc[i], wa_w, wa_s, z, i)
+
+        def first_layer(i):
             b = bank("b", i, [P, R])
             for z in range(PASSES):
                 nc.tensor.matmul_mx(
@@ -178,8 +180,10 @@ def tile_moe_expert_hidden_gated_pair_kernel(
                     rhs=wc_w[:, z, :].bitcast(FP8X4), rhs_scale=wc_s[ROWS * z : P, :],
                     start=(z == 0), stop=(z == PASSES - 1),
                 )
+            if i + A_LEAD < BLOCKS:
+                product_a(i + A_LEAD)
             a_term = ring.tile([P, PACK, P], F32, name="a_term")
-            nc.vector.scalar_tensor_tensor(out=a_term[:], in0=gate[i][:], scalar=-1.0, in1=by_t(a), op0=MULT, op1=MULT)
+            nc.vector.scalar_tensor_tensor(out=a_term[:], in0=gate[i][:], scalar=-1.0, in1=by_t(a_acc[i]), op0=MULT, op1=MULT)
             b_term = ring.tile([P, PACK, P], F32, name="b_term")
             nc.vector.scalar_tensor_tensor(out=b_term[:], in0=gate[i][:], scalar=1.0, in1=by_t(b), op0=SUBTRACT, op1=MULT)
             terms[i] = (a_term, b_term)
@@ -223,6 +227,8 @@ def tile_moe_expert_hidden_gated_pair_kernel(
                 )
                 queue.dma_start(out=out_tiles[:, tiles, slots(i)], in_=y[:])
 
+        for i in range(A_LEAD):
+            product_a(i)
         for step in range(BLOCKS + SECOND_LAG):
             if step < BLOCKS:
                 first_layer(step)

from contextlib import ExitStack

import concourse.mybir as mybir
from concourse.masks import make_identity

K, T, J, R, N = 1024, 1024, 512, 512, 512
FLOPS = 2 * (3 * K * R * J + R * N * J)

F32 = mybir.dt.float32
BF16 = mybir.dt.bfloat16
I32 = mybir.dt.int32
U32 = mybir.dt.uint32
U16 = mybir.dt.uint16
U8 = mybir.dt.uint8
FP8X4 = mybir.dt.float8_e4m3fn_x4
FP4X4 = mybir.dt.float4_e2m1fn_x4
MULT = mybir.AluOpType.mult
SUBTRACT = mybir.AluOpType.subtract
SIGMOID = mybir.ActivationFunctionType.Sigmoid

P = 128
PACK = 4
PASSES = K // (P * PACK)
QUADRANTS = 4
ROWS = 4
BLOCKS = J // P
HALF = J // 2
OUT_TILES = N // P
LIFTED = 112
SECOND_LAG = 3
A_LEAD = 2


def tile_moe_expert_hidden_gated_pair_kernel(
    tc, xt_words, xt_scales, wa_words, wa_scales, wc_words, wc_scales, wg_words, wg_scales,
    us, wb_words, wb_scales, rw, offs, offs2, out,
):
    nc = tc.nc
    with ExitStack() as ctx:
        keep = ctx.enter_context(tc.tile_pool(name="keep", bufs=1))
        ring = ctx.enter_context(tc.tile_pool(name="ring", bufs=BLOCKS))
        psum = ctx.enter_context(tc.psum_pool(name="psum", bufs=1))

        def held(name, shape, dtype):
            return keep.tile(shape, dtype, name=name, align_bytes=64)

        def bank(name, number, shape):
            return psum.tile(shape, F32, name=name, tag="bank%d" % number)

        list1 = held("list1", [P, J // 16], U16)
        list2 = held("list2", [P, J // 16], U16)
        x_words = held("x_words", [P, PASSES * T], I32)
        x_scales = held("x_scales", [P, T], U8)
        wa_w = held("wa_w", [P, PASSES, 2 * R], U8)
        wg_w = held("wg_w", [P, PASSES, 2 * R], U8)
        wc_w = held("wc_w", [P, PASSES, R], I32)
        wb_w = held("wb_w", [P, N], I32)
        wa_s = held("wa_s", [P, PASSES, R], U8)
        wg_s = held("wg_s", [P, PASSES, R], U8)
        wc_s = held("wc_s", [P, R], U8)
        wb_s = held("wb_s", [P, N], U8)
        token_s = held("token_s", [P, J], U8)
        token_s_pass1 = held("token_s_pass1", [P, J], U8)
        context_s = held("context_s", [P, J], U8)
        us_sb = held("us_sb", [P, PACK], F32)
        rw_all = held("rw_all", [P, J], F32)
        ident = held("ident", [P, P], F32)

        nc.gpsimd.memset(x_scales[:].bitcast(I32), 0)
        nc.vector.memset(wc_s[:].bitcast(I32), 0)
        for tile in (wg_s, wa_s):
            nc.vector.memset(tile[:].rearrange("p z c -> p (z c)").bitcast(I32), 0)
        for tile in (token_s_pass1, wb_s):
            nc.vector.memset(tile[:].bitcast(I32), 0)
        make_identity(nc, ident[:])

        def load_stacked(queue, tile, scales, q):
            queue.dma_start(
                out=tile[32 * q : 32 * q + ROWS * scales.shape[0], :].bitcast(I32),
                in_=scales[:, ROWS * q : ROWS * (q + 1), :].bitcast(I32),
            )

        def load_beside(tile, scales, q):
            nc.sync.dma_start(
                out=tile[32 * q : 32 * q + ROWS, :, :].bitcast(I32),
                in_=scales[:, ROWS * q : ROWS * (q + 1), :].rearrange("z q c -> q z c").bitcast(I32),
            )

        def load_x_pass(z):
            nc.sync.dma_start(
                out=x_words[:, z * T : (z + 1) * T], in_=xt_words[z].rearrange("p n t -> p (n t)").bitcast(I32)
            )

        def load_fp4(tile, words):
            nc.sync.dma_start(out=tile[:].bitcast(I32), in_=words.rearrange("z p c -> p z c").bitcast(I32))

        for q in range(QUADRANTS):
            load_stacked(nc.sync, x_scales, xt_scales, q)
        nc.sync.dma_start(list1[:], offs)
        load_x_pass(0)
        nc.sync.dma_start(list2[:], offs2)
        load_fp4(wg_w, wg_words)
        for q in range(QUADRANTS):
            load_beside(wg_s, wg_scales, q)
        load_x_pass(1)
        load_fp4(wa_w, wa_words)
        for q in range(QUADRANTS):
            load_stacked(nc.gpsimd, wc_s, wc_scales, q)

        nc.vector.tensor_copy(token_s[:], x_scales[:].indirect(list1[:]))
        nc.sync.dma_start(out=token_s_pass1[0:LIFTED, :].bitcast(I32), in_=token_s[ROWS : ROWS + LIFTED, :].bitcast(I32))

        for q in range(QUADRANTS):
            load_beside(wa_s, wa_scales, q)
        nc.sync.dma_start(out=wc_w[:], in_=wc_words.rearrange("z p n t -> p z (n t)").bitcast(I32))
        nc.sync.dma_start(out=us_sb[:], in_=us.rearrange("(p t) o -> p (t o)", t=PACK))
        nc.sync.dma_start(out=wb_w[:], in_=wb_words[0].rearrange("p n t -> p (n t)").bitcast(I32))
        for q in range(QUADRANTS):
            load_stacked(nc.sync, wb_s, wb_scales, q)
        nc.sync.dma_start(out=rw_all[:], in_=rw[0].partition_broadcast(P))

        def gather_words(name, offsets, window, half):
            words = held(name, [P, HALF], I32)
            columns = HALF // 16
            nc.vector.tensor_copy(
                words[:].bitcast(U32), window.bitcast(U32).indirect(offsets[:, half * columns : (half + 1) * columns])
            )
            return words

        token_w = {}
        context_w = {}
        for half in range(2):
            token_w[0, half] = gather_words("token_w0%d" % half, list1, x_words[:, 0:T], half)
        nc.vector.tensor_copy(context_s[:], x_scales[:].indirect(list2[:]))
        for half in range(2):
            token_w[1, half] = gather_words("token_w1%d" % half, list1, x_words[:, T : 2 * T], half)
        for half in range(2):
            context_w[0, half] = gather_words("context_w0%d" % half, list2, x_words[:], half)
            context_w[1, half] = gather_words("context_w1%d" % half, list2, x_words[:, T : 2 * T], half)

        def slots(i):
            return slice(i * P, (i + 1) * P)

        def stationary(words, z, i):
            return words[z, i // 2][:, slots(i % 2)].bitcast(FP8X4)

        def fp4_pass(acc, w, w_s, z, i):
            nc.tensor.matmul_mx(
                out=acc[:], lhsT=stationary(token_w, z, i), lhsT_scale=(token_s, token_s_pass1)[z][:, slots(i)],
                rhs=w[:, z, :].bitcast(FP4X4), rhs_scale=w_s[:, z, :], start=(z == 0), stop=(z == PASSES - 1),
            )

        def by_t(acc):
            return acc[:].rearrange("p (m t) -> p t m", t=PACK)

        g_acc = [bank("g", i, [P, R]) for i in range(BLOCKS)]
        gate = []
        for i in range(BLOCKS):
            fp4_pass(g_acc[i], wg_w, wg_s, 0, i)
        for i in range(BLOCKS):
            fp4_pass(g_acc[i], wg_w, wg_s, 1, i)
            s = ring.tile([P, PACK, P], F32, name="s")
            nc.scalar.activation(out=s[:], in_=by_t(g_acc[i]), func=SIGMOID)
            gate.append(s)

        a_acc = {}
        terms = {}
        quantised = {}

        def product_a(i):
            a_acc[i] = bank("a", BLOCKS + i, [P, R])
            for z in range(PASSES):
                fp4_pass(a_acc[i], wa_w, wa_s, z, i)

        def first_layer(i):
            b = bank("b", i, [P, R])
            for z in range(PASSES):
                nc.tensor.matmul_mx(
                    out=b[:], lhsT=stationary(context_w, z, i), lhsT_scale=context_s[ROWS * z : P, slots(i)],
                    rhs=wc_w[:, z, :].bitcast(FP8X4), rhs_scale=wc_s[ROWS * z : P, :],
                    start=(z == 0), stop=(z == PASSES - 1),
                )
            if i + A_LEAD < BLOCKS:
                product_a(i + A_LEAD)
            a_term = ring.tile([P, PACK, P], F32, name="a_term")
            nc.vector.scalar_tensor_tensor(out=a_term[:], in0=gate[i][:], scalar=-1.0, in1=by_t(a_acc[i]), op0=MULT, op1=MULT)
            b_term = ring.tile([P, PACK, P], F32, name="b_term")
            nc.vector.scalar_tensor_tensor(out=b_term[:], in0=gate[i][:], scalar=1.0, in1=by_t(b), op0=SUBTRACT, op1=MULT)
            terms[i] = (a_term, b_term)

        def hidden(i):
            turned = bank("turned", BLOCKS + i, [P, PACK, P])
            for n_term, term in enumerate(terms[i]):
                for t in range(PACK):
                    nc.tensor.matmul(
                        turned[:, t, :], term[:, t, :], ident[:], is_transpose=True,
                        start=(n_term == 0 and t == 0), stop=(n_term == 1 and t == PACK - 1),
                    )
            hid = ring.tile([P, P, PACK], BF16, name="hid", align_bytes=64)
            nc.vector.scalar_tensor_tensor(
                out=hid[:], in0=turned[:].rearrange("p t j -> p j t"), scalar=-1.0,
                in1=us_sb[:].unsqueeze(1).to_broadcast([P, P, PACK]), op0=MULT, op1=MULT,
            )
            codes = ring.tile([P, P], U32, name="codes", align_bytes=64)
            scales = ring.tile([P, P], U8, name="scales", align_bytes=64)
            nc.vector.quantize_mx(out=codes[:].bitcast(FP8X4), scales=scales[:], in_=hid[:].rearrange("p j t -> p (j t)"))
            quantised[i] = (codes, scales)

        out_tiles = out.rearrange("(nb p) j -> p nb j", p=P)

        def second_layer(i):
            codes, scales = quantised[i]
            sums = bank("sums", i, [P, OUT_TILES, P])
            for nb in range(OUT_TILES):
                nc.tensor.matmul_mx(
                    out=sums[:, nb, :], lhsT=wb_w[:, slots(nb)].bitcast(FP8X4), lhsT_scale=wb_s[:, slots(nb)],
                    rhs=codes[:].bitcast(FP8X4), rhs_scale=scales[:], start=True, stop=True,
                )
            queues = (nc.sync, nc.scalar) if i == BLOCKS - 1 else (nc.sync,)
            width = OUT_TILES // len(queues)
            for part, queue in enumerate(queues):
                tiles = slice(part * width, (part + 1) * width)
                y = ring.tile([P, width, P], F32, name="y%d" % part)
                nc.vector.tensor_tensor(
                    out=y[:], in0=sums[:, tiles, :], in1=rw_all[:, slots(i)].unsqueeze(1).to_broadcast([P, width, P]),
                    op=MULT,
                )
                queue.dma_start(out=out_tiles[:, tiles, slots(i)], in_=y[:])

        for i in range(A_LEAD):
            product_a(i)
        for step in range(BLOCKS + SECOND_LAG):
            if step < BLOCKS:
                first_layer(step)
            if 1 <= step <= BLOCKS:
                hidden(step - 1)
            if step >= SECOND_LAG:
                second_layer(step - SECOND_LAG)
